import numpy as np
import ml_dtypes


def mxq(x, axis, fmt="e4m3"):
    dtype, down = {"e4m3": (ml_dtypes.float8_e4m3fn, 7), "e5m2": (ml_dtypes.float8_e5m2, 14)}[fmt]
    v = np.moveaxis(np.asarray(x, np.float32).astype(ml_dtypes.bfloat16).astype(np.float64), axis, -1)
    blocks = v.reshape(v.shape[:-1] + (-1, 32))
    amax = np.abs(blocks).max(-1, keepdims=True)
    byte = np.maximum(np.where(amax > 0, np.frexp(amax)[1] - 1 + 127, 0) - down, 1)
    scale = np.exp2(byte - 127.0)
    codes = (blocks / scale).astype(np.float32).astype(dtype).astype(np.float64)
    return np.moveaxis((codes * scale).reshape(v.shape), -1, axis)


WIDE = False


def mx_kscale(k):
    if not WIDE:
        return np.ones(k)
    levels = np.array([10, -10, 5, -5, 0])
    if k % 512:
        return np.exp2(np.random.permutation(np.resize(levels, k // 32))).repeat(32)
    a = np.empty((k // 512, 16))
    for p in range(k // 512):
        a[p, :8] = np.random.permutation(np.resize(levels, 8))
        for g in range(8):
            far = levels[np.abs(levels - a[p, g]) >= 10]
            a[p, g + 8] = far[np.random.randint(len(far))]
    return np.exp2(a.ravel()).repeat(32)


def f64(x):
    return np.asarray(x).astype(np.float64)


def striped(idx):
    return np.tile(idx.reshape(-1, 16).T, (8, 1)).astype(np.uint16)


def unstriped(offs):
    return offs[:16].T.reshape(-1).astype(np.int64)


def pack_weight(w):
    k, n = w.shape
    w = f64(np.asarray(w, np.float32).astype(ml_dtypes.bfloat16)).reshape(k // 32, 32, n)
    amax = np.abs(w).max(1)
    byte = np.clip(np.where(amax > 0, np.frexp(amax)[1] - 1 + 127 - 7, 1), 1, 254)
    scaled = (w * np.exp2(127.0 - byte)[:, None, :]).reshape(k, n).astype(np.float32)
    words = np.ascontiguousarray(scaled.reshape(k // 512, 128, 4, n).transpose(0, 1, 3, 2)).astype(ml_dtypes.float8_e4m3fn).view(np.uint8)
    return words, np.ascontiguousarray(byte.astype(np.uint8).reshape(k // 512, 16, n))


def unpack_weight(words, scales):
    g, p, n, _ = words.shape
    vals = np.ascontiguousarray(words).view(ml_dtypes.float8_e4m3fn).astype(np.float64) * np.repeat(np.exp2(scales.astype(np.float64) - 127.0), 8, axis=1)[..., None]
    return vals.transpose(0, 1, 3, 2).reshape(g * 512, n)


K, T, S, H, V, W, G = 512, 1024, 512, 512, 512, 1024, 2048
P = 2 ** 7


def setup_inputs():
    n = np.random.standard_normal
    s = mx_kscale(K)[:, None]
    u = mx_kscale(H)
    packed_xT = pack_weight(n((K, T)) * s)
    packed_eT = pack_weight(n((K, W)) * s)
    packed_vT = pack_weight(n((H, G)) / np.sqrt(H) / u[:, None])
    return {
        "x_words": packed_xT[0],
        "x_scales": packed_xT[1],
        "e_words": packed_eT[0],
        "e_scales": packed_eT[1],
        "w1": (n((K, H)) / np.sqrt(2 * K) / s * u).astype(np.float32),
        "w2": (n((K, H)) / np.sqrt(2 * K) / s * u).astype(np.float32),
        "v_words": packed_vT[0],
        "v_scales": packed_vT[1],
        "half": (np.tile(np.random.uniform(0.3, 1.0, G), (P, 1))).astype(np.float32),
        "offs": striped(np.random.permutation(T)[:S]),
        "code": striped(np.random.permutation(W)[:S]),
        "cand": striped(np.random.permutation(G)[:V]),
    }


def reference(x_words, x_scales, e_words, e_scales, w1, w2, v_words, v_scales, half, offs, code, cand):
    xq = unpack_weight(x_words, x_scales)[:, unstriped(offs)]
    e_code = unpack_weight(e_words, e_scales)[:, unstriped(code)]
    y = mxq(f64(w2), 0, "e4m3").T @ e_code
    rr = (mxq(f64(w1), 0, "e4m3").T @ xq) - y
    v_cand = unpack_weight(v_words, v_scales)[:, unstriped(cand)]
    return (mxq(rr, 0, "e4m3").T @ v_cand) - (f64(half)[:1][:, unstriped(cand)])

@@ -1,0 +1,174 @@
+from contextlib import ExitStack
+
+import concourse.mybir as mybir
+from concourse.masks import make_identity
+
+F32 = mybir.dt.float32
+BF16 = mybir.dt.bfloat16
+I32 = mybir.dt.int32
+U32 = mybir.dt.uint32
+U16 = mybir.dt.uint16
+U8 = mybir.dt.uint8
+FP8X4 = mybir.dt.float8_e4m3fn_x4
+COPY = mybir.ActivationFunctionType.Copy
+SUB = mybir.AluOpType.subtract
+
+P = 128
+PACK = 4
+K, T, S, H, V, W, G = 512, 1024, 512, 512, 512, 1024, 2048
+FLOPS = 2 * (2 * K * H * S + H * S * V)
+BYTES = K * (T + W + G) + (K // 32) * (T + W + G) + 2 * 4 * K * H + 4 * G + 3 * 2 * P * 32 + 4 * S * V
+
+
+def tile_picked_yrvq_score_p_kernel(
+    tc, x_words, x_scales, e_words, e_scales, w1, w2, v_words, v_scales, half, offs, code, cand, out
+):
+    nc = tc.nc
+    with ExitStack() as ctx:
+        lists = ctx.enter_context(tc.tile_pool(name="lists", bufs=1))
+        keep = ctx.enter_context(tc.tile_pool(name="keep", bufs=1))
+        psum = ctx.enter_context(tc.psum_pool(name="psum", bufs=1))
+
+        def sb(name, shape, dtype, tag=None):
+            return keep.tile(shape, dtype, name=name, tag=tag or name, align_bytes=64)
+
+        offs_t = lists.tile([P, S // 16], U16, name="offs_t")
+        code_t = lists.tile([P, S // 16], U16, name="code_t")
+        cand_t = lists.tile([P, V // 16], U16, name="cand_t")
+
+        xs_win = sb("xs_win", [P, T], U8)
+        es_win = sb("es_win", [P, W], U8)
+        vs_win = sb("vs_win", [P, G], U8)
+        h_win = sb("h_win", [P, G], F32)
+        xw_win = sb("xw_win", [P, T], U32)
+        ew_win = sb("ew_win", [P, W], U32)
+        vw_win = sb("vw_win", [P, G], U32)
+        planes = sb("planes", [P, 3, S], U8)
+        raw = [[sb("raw%d%d" % (a, b), [P, PACK, H // 2], F32) for b in range(2)] for a in range(2)]
+
+        def load_scales(queue, win, scales):
+            queue.dma_start(win[0:16, :].bitcast(I32), scales[0].bitcast(I32))
+
+        def load_words(win, words):
+            nc.sync.dma_start(win[:].bitcast(I32), words[0].rearrange("p n t -> p (n t)").bitcast(I32))
+
+        def load_w(a, b, queue=nc.sync):
+            w = (w1, w2)[a].rearrange("(p j) c -> p j c", j=PACK)
+            queue.dma_start(raw[a][b][:], w[:, :, b * (H // 2) : (b + 1) * (H // 2)])
+
+        for win in (xs_win, es_win, vs_win):
+            nc.gpsimd.memset(win[:].bitcast(I32), 0)
+        nc.vector.memset(h_win[:], 0.0)
+        nc.gpsimd.memset(planes[:].rearrange("p a s -> p (a s)").bitcast(I32), 0)
+        ident = sb("ident", [P, P], F32)
+        make_identity(nc, ident[:])
+
+        nc.sync.dma_start(offs_t[:], offs)
+        load_scales(nc.scalar, xs_win, x_scales)
+        load_w(0, 0)
+        load_scales(nc.scalar, es_win, e_scales)
+        nc.sync.dma_start(code_t[:], code)
+        nc.sync.dma_start(cand_t[:], cand)
+        load_scales(nc.scalar, vs_win, v_scales)
+        load_w(0, 1)
+        nc.sync.dma_start(h_win[0:1, :], half[0:1, :])
+        load_w(1, 0)
+        load_w(1, 1)
+        load_words(xw_win, x_words)
+        load_words(ew_win, e_words)
+
+        picked = sb("picked", [P, 3, S], U8)
+        hg = sb("hg", [P, V], F32)
+        xw = sb("xw", [P, S], U32)
+        ew = sb("ew", [P, S], U32)
+        vw = sb("vw", [P, V], U32)
+        grouped = [sb("grouped%d" % a, [P, PACK * H], BF16) for a in range(2)]
+        wq = [sb("wq%d" % a, [P, H], U32) for a in range(2)]
+        wsc = [sb("wsc%d" % a, [P, H], U8) for a in range(2)]
+
+        def gather(dst, win, lst):
+            nc.vector.tensor_copy(dst, win[:].indirect(lst))
+
+        def cast_w(a, b):
+            half_m = P // 2
+            dst = grouped[a][:].rearrange("p (t m j) -> p m t j", t=PACK, j=PACK)[:, b * half_m : (b + 1) * half_m]
+            src = raw[a][b][:].rearrange("p j (m t) -> p m t j", t=PACK)
+            nc.scalar.activation(dst, src, COPY, scale=(1.0, -1.0)[a])
+
+        def quant_w(a):
+            nc.vector.quantize_mx(out=wq[a][:].bitcast(FP8X4), scales=wsc[a][:], in_=grouped[a][:])
+
+        gather(picked[:, 0, :], xs_win, offs_t[:])
+        cast_w(0, 0)
+        gather(picked[:, 1, :], es_win, code_t[:])
+        cast_w(0, 1)
+        gather(picked[:, 2, :], vs_win, cand_t[:])
+        for q in range(4):
+            nc.sync.dma_start(
+                planes[32 * q : 32 * q + 4].rearrange("p a s -> p (a s)").bitcast(I32),
+                picked[4 * q : 4 * q + 4].rearrange("p a s -> p (a s)").bitcast(I32),
+            )
+        load_words(vw_win, v_words)
+        gather(hg[:], h_win, cand_t[:])
+        cast_w(1, 0)
+        quant_w(0)
+        cast_w(1, 1)
+        gather(xw[:], xw_win, offs_t[:])
+        quant_w(1)
+        for b in range(2):
+            gather(ew[:, b * 256 : (b + 1) * 256], ew_win, code_t[:, b * 16 : (b + 1) * 16])
+
+        h_turn = psum.tile([P, PACK, P], F32, name="h_turn", tag="o2")
+        for c in range(4):
+            nc.tensor.transpose(h_turn[:, c, :], hg[:, c * P : (c + 1) * P], ident[:])
+        h_col = sb("h_col", [P, 4], F32, tag="raw11")
+        nc.scalar.copy(h_col[:], h_turn[:, :, 0])
+        h_bank = psum.tile([P, V], F32, name="h_bank", tag="o3")
+        for c in range(4):
+            nc.tensor.transpose(h_bank[:, c * P : (c + 1) * P], h_col[:, c : c + 1].to_broadcast([P, P]), ident[:])
+        hb = sb("hb", [P, V], F32)
+        nc.scalar.copy(hb[:], h_bank[:])
+
+        rr_bf = []
+        banks = []
+
+        def first(tt):
+            cols = slice(tt * P, (tt + 1) * P)
+            bank = psum.tile([P, PACK, P], F32, name="rr_bank%d" % tt)
+            for j in range(PACK):
+                wc = slice(j * P, (j + 1) * P)
+                nc.tensor.matmul_mx(out=bank[:, j, :], lhsT=wq[0][:, wc].bitcast(FP8X4), lhsT_scale=wsc[0][:, wc],
+                                    rhs=xw[:, cols].bitcast(FP8X4), rhs_scale=planes[:, 0, cols], start=True, stop=False)
+                nc.tensor.matmul_mx(out=bank[:, j, :], lhsT=wq[1][:, wc].bitcast(FP8X4), lhsT_scale=wsc[1][:, wc],
+                                    rhs=ew[:, cols].bitcast(FP8X4), rhs_scale=planes[:, 1, cols], start=False, stop=True)
+            rb = sb("rr_bf%d" % tt, [P, P, PACK], BF16)
+            nc.scalar.copy(rb[:], bank[:].rearrange("p j n -> p n j"))
+            rr_bf.append(rb)
+
+        def second(tt):
+            rq = sb("rq%d" % tt, [P, P], U32)
+            rs = sb("rs%d" % tt, [P, P], U8)
+            nc.vector.quantize_mx(out=rq[:].bitcast(FP8X4), scales=rs[:], in_=rr_bf[tt][:].rearrange("p n j -> p (n j)"))
+            ob = psum.tile([P, V], F32, name="o_bank%d" % tt, tag="o%d" % tt)
+            nc.tensor.matmul_mx(out=ob[:], lhsT=rq[:].bitcast(FP8X4), lhsT_scale=rs[:],
+                                rhs=vw[:].bitcast(FP8X4), rhs_scale=planes[:, 2, :], start=True, stop=True)
+            banks.append(ob)
+
+        def finish(tt):
+            res = sb("res%d" % tt, [P, V], F32, tag="rr_bf%d" % ((tt + 1) % 4))
+            nc.vector.tensor_tensor(res[:], banks[tt][:], hb[:], SUB)
+            nc.sync.dma_start(out[tt * P : (tt + 1) * P, :], res[:])
+
+        first(0)
+        first(1)
+        gather(vw[:], vw_win, cand_t[:])
+        second(0)
+        first(2)
+        second(1)
+        finish(0)
+        first(3)
+        second(2)
+        finish(1)
+        second(3)
+        finish(2)
+        finish(3)

@@ -71,8 +71,8 @@ def tile_picked_yrvq_score_p_kernel(
         nc.sync.dma_start(cand_t[:], cand)
         load_scales(nc.scalar, vs_win, v_scales)
         load_w(0, 1)
-        nc.sync.dma_start(h_win[0:1, :], half[0:1, :])
         load_w(1, 0)
+        nc.sync.dma_start(h_win[0:1, :], half[0:1, :])
         load_w(1, 1)
         load_words(xw_win, x_words)
         load_words(ew_win, e_words)
@@ -146,11 +146,11 @@ def tile_picked_yrvq_score_p_kernel(
             rr_bf.append(rb)
 
         def second(tt):
-            rq = sb("rq%d" % tt, [P, P], U32)
+            rq = rq_all[:, tt * P : (tt + 1) * P]
             rs = sb("rs%d" % tt, [P, P], U8)
-            nc.vector.quantize_mx(out=rq[:].bitcast(FP8X4), scales=rs[:], in_=rr_bf[tt][:].rearrange("p n j -> p (n j)"))
+            nc.vector.quantize_mx(out=rq.bitcast(FP8X4), scales=rs[:], in_=rr_bf[tt][:].rearrange("p n j -> p (n j)"))
             ob = psum.tile([P, V], F32, name="o_bank%d" % tt, tag="o%d" % tt)
-            nc.tensor.matmul_mx(out=ob[:], lhsT=rq[:].bitcast(FP8X4), lhsT_scale=rs[:],
+            nc.tensor.matmul_mx(out=ob[:], lhsT=rq.bitcast(FP8X4), lhsT_scale=rs[:],
                                 rhs=vw[:].bitcast(FP8X4), rhs_scale=planes[:, 2, :], start=True, stop=True)
             banks.append(ob)
 
@@ -162,6 +162,7 @@ def tile_picked_yrvq_score_p_kernel(
         first(0)
         first(1)
         gather(vw[:], vw_win, cand_t[:])
+        rq_all = sb("rq_all", [P, S], U32, tag="vw_win")
         second(0)
         first(2)
         second(1)

@@ -1,7 +1,6 @@
 from contextlib import ExitStack
 
 import concourse.mybir as mybir
-from concourse.masks import make_identity
 
 F32 = mybir.dt.float32
 BF16 = mybir.dt.bfloat16
@@ -60,8 +59,6 @@ def tile_picked_yrvq_score_p_kernel(
             nc.gpsimd.memset(win[:].bitcast(I32), 0)
         nc.vector.memset(h_win[:], 0.0)
         nc.gpsimd.memset(planes[:].rearrange("p a s -> p (a s)").bitcast(I32), 0)
-        ident = sb("ident", [P, P], F32)
-        make_identity(nc, ident[:])
 
         nc.sync.dma_start(offs_t[:], offs)
         load_scales(nc.scalar, xs_win, x_scales)
@@ -72,7 +69,7 @@ def tile_picked_yrvq_score_p_kernel(
         load_scales(nc.scalar, vs_win, v_scales)
         load_w(0, 1)
         load_w(1, 0)
-        nc.sync.dma_start(h_win[0:1, :], half[0:1, :])
+        nc.sync.dma_start(h_win[0:32:4, :], half[0:8, :])
         load_w(1, 1)
         load_words(xw_win, x_words)
         load_words(ew_win, e_words)
@@ -91,8 +88,8 @@ def tile_picked_yrvq_score_p_kernel(
 
         def cast_w(a, b):
             half_m = P // 2
-            dst = grouped[a][:].rearrange("p (t m j) -> p m t j", t=PACK, j=PACK)[:, b * half_m : (b + 1) * half_m]
-            src = raw[a][b][:].rearrange("p j (m t) -> p m t j", t=PACK)
+            dst = grouped[a][:].rearrange("p (t m j) -> p m j t", t=PACK, j=PACK)[:, b * half_m : (b + 1) * half_m]
+            src = raw[a][b][:].rearrange("p j (m t) -> p m j t", t=PACK)
             nc.scalar.activation(dst, src, COPY, scale=(1.0, -1.0)[a])
 
         def quant_w(a):
@@ -115,38 +112,44 @@ def tile_picked_yrvq_score_p_kernel(
         cast_w(1, 1)
         gather(xw[:], xw_win, offs_t[:])
         quant_w(1)
-        for b in range(2):
-            gather(ew[:, b * 256 : (b + 1) * 256], ew_win, code_t[:, b * 16 : (b + 1) * 16])
+        gather(ew[:, 0:128], ew_win, code_t[:, 0:8])
+        gather(ew[:, 128:512], ew_win, code_t[:, 8:32])
 
-        h_turn = psum.tile([P, PACK, P], F32, name="h_turn", tag="o2")
-        for c in range(4):
-            nc.tensor.transpose(h_turn[:, c, :], hg[:, c * P : (c + 1) * P], ident[:])
-        h_col = sb("h_col", [P, 4], F32, tag="raw11")
-        nc.scalar.copy(h_col[:], h_turn[:, :, 0])
-        h_bank = psum.tile([P, V], F32, name="h_bank", tag="o3")
-        for c in range(4):
-            nc.tensor.transpose(h_bank[:, c * P : (c + 1) * P], h_col[:, c : c + 1].to_broadcast([P, P]), ident[:])
         hb = sb("hb", [P, V], F32)
-        nc.scalar.copy(hb[:], h_bank[:])
+        nc.sync.dma_start(hb[:], hg[0:32:4, :].unsqueeze(1).broadcast_to([8, 16, V]))
 
         rr_bf = []
         banks = []
 
-        def first(tt):
+        rr_banks = [psum.tile([P, PACK, P], F32, name="rr_bank%d" % tt) for tt in range(4)]
+
+        def x_pass(tt, j):
             cols = slice(tt * P, (tt + 1) * P)
-            bank = psum.tile([P, PACK, P], F32, name="rr_bank%d" % tt)
+            wc = slice(j * P, (j + 1) * P)
+            nc.tensor.matmul_mx(out=rr_banks[tt][:, j, :], lhsT=wq[0][:, wc].bitcast(FP8X4), lhsT_scale=wsc[0][:, wc],
+                                rhs=xw[:, cols].bitcast(FP8X4), rhs_scale=planes[:, 0, cols], start=True, stop=False)
+
+        def e_pass(tt, j):
+            cols = slice(tt * P, (tt + 1) * P)
+            wc = slice(j * P, (j + 1) * P)
+            nc.tensor.matmul_mx(out=rr_banks[tt][:, j, :], lhsT=wq[1][:, wc].bitcast(FP8X4), lhsT_scale=wsc[1][:, wc],
+                                rhs=ew[:, cols].bitcast(FP8X4), rhs_scale=planes[:, 1, cols], start=False, stop=True)
+
+        for tt in range(4):
+            x_pass(tt, 0)
+
+        def first(tt):
+            bank = rr_banks[tt]
             for j in range(PACK):
-                wc = slice(j * P, (j + 1) * P)
-                nc.tensor.matmul_mx(out=bank[:, j, :], lhsT=wq[0][:, wc].bitcast(FP8X4), lhsT_scale=wsc[0][:, wc],
-                                    rhs=xw[:, cols].bitcast(FP8X4), rhs_scale=planes[:, 0, cols], start=True, stop=False)
-                nc.tensor.matmul_mx(out=bank[:, j, :], lhsT=wq[1][:, wc].bitcast(FP8X4), lhsT_scale=wsc[1][:, wc],
-                                    rhs=ew[:, cols].bitcast(FP8X4), rhs_scale=planes[:, 1, cols], start=False, stop=True)
+                if j > 0:
+                    x_pass(tt, j)
+                e_pass(tt, j)
             rb = sb("rr_bf%d" % tt, [P, P, PACK], BF16)
             nc.scalar.copy(rb[:], bank[:].rearrange("p j n -> p n j"))
             rr_bf.append(rb)
 
         def second(tt):
-            rq = rq_all[:, tt * P : (tt + 1) * P]
+            rq = rq_all[:, (tt % 2) * P : (tt % 2 + 1) * P]
             rs = sb("rs%d" % tt, [P, P], U8)
             nc.vector.quantize_mx(out=rq.bitcast(FP8X4), scales=rs[:], in_=rr_bf[tt][:].rearrange("p n j -> p (n j)"))
             ob = psum.tile([P, V], F32, name="o_bank%d" % tt, tag="o%d" % tt)
@@ -162,7 +165,7 @@ def tile_picked_yrvq_score_p_kernel(
         first(0)
         first(1)
         gather(vw[:], vw_win, cand_t[:])
-        rq_all = sb("rq_all", [P, S], U32, tag="vw_win")
+        rq_all = sb("rq_all", [P, 2 * P], U32, tag="vw_win")
         second(0)
         first(2)
         second(1)

@@ -43,77 +43,79 @@ def tile_picked_yrvq_score_p_kernel(
         ew_win = sb("ew_win", [P, W], U32)
         vw_win = sb("vw_win", [P, G], U32)
         planes = sb("planes", [P, 3, S], U8)
-        raw = [[sb("raw%d%d" % (a, b), [P, PACK, H // 2], F32) for b in range(2)] for a in range(2)]
+        raw = [sb("raw%d" % a, [P, PACK, H], F32) for a in range(2)]
 
         def load_scales(queue, win, scales):
-            queue.dma_start(win[0:16, :].bitcast(I32), scales[0].bitcast(I32))
+            queue.dma_start(win[4:P:8, :].bitcast(I32), scales[0].bitcast(I32))
 
-        def load_words(win, words):
-            nc.sync.dma_start(win[:].bitcast(I32), words[0].rearrange("p n t -> p (n t)").bitcast(I32))
+        def load_words(win, words, cols=slice(None)):
+            nc.sync.dma_start(win[:, cols].bitcast(I32), words[0].rearrange("p n t -> p (n t)").bitcast(I32)[:, cols])
 
-        def load_w(a, b, queue=nc.sync):
+        def load_w(a, rows):
             w = (w1, w2)[a].rearrange("(p j) c -> p j c", j=PACK)
-            queue.dma_start(raw[a][b][:], w[:, :, b * (H // 2) : (b + 1) * (H // 2)])
+            nc.sync.dma_start(raw[a][:, rows, :], w[:, rows, :])
 
         for win in (xs_win, es_win, vs_win):
-            nc.gpsimd.memset(win[:].bitcast(I32), 0)
-        nc.vector.memset(h_win[:], 0.0)
-        nc.gpsimd.memset(planes[:].rearrange("p a s -> p (a s)").bitcast(I32), 0)
+            nc.vector.memset(win[:].bitcast(I32), 0)
+        nc.vector.memset(h_win[0:64, G - 8 : G], 0.0)
+        nc.vector.memset(h_win[:, 0 : G - 8], 0.0)
+        nc.vector.memset(planes[:].rearrange("p a s -> p (a s)").bitcast(I32), 0)
 
         nc.sync.dma_start(offs_t[:], offs)
-        load_scales(nc.scalar, xs_win, x_scales)
-        load_w(0, 0)
-        load_scales(nc.scalar, es_win, e_scales)
+        load_w(0, slice(0, 1))
+        load_scales(nc.sync, xs_win, x_scales)
+        load_scales(nc.sync, es_win, e_scales)
         nc.sync.dma_start(code_t[:], code)
-        nc.sync.dma_start(cand_t[:], cand)
         load_scales(nc.scalar, vs_win, v_scales)
-        load_w(0, 1)
-        load_w(1, 0)
-        nc.sync.dma_start(h_win[0:32:4, :], half[0:8, :])
-        load_w(1, 1)
+        load_w(0, slice(1, PACK))
+        nc.scalar.dma_start(h_win[0:32:4, :], half[0:8, :])
+        nc.scalar.activation(h_win[64:P, G - 8 : G], h_win[64:P, 0:8], COPY)
+        nc.sync.dma_start(cand_t[:], cand)
+        load_w(1, slice(0, PACK))
         load_words(xw_win, x_words)
         load_words(ew_win, e_words)
 
-        picked = sb("picked", [P, 3, S], U8)
+        picked = sb("picked", [P, 2, S], U8)
+        picked_v = sb("picked_v", [P, V], U8)
         hg = sb("hg", [P, V], F32)
         xw = sb("xw", [P, S], U32)
         ew = sb("ew", [P, S], U32)
         vw = sb("vw", [P, V], U32)
         grouped = [sb("grouped%d" % a, [P, PACK * H], BF16) for a in range(2)]
-        wq = [sb("wq%d" % a, [P, H], U32) for a in range(2)]
+        wq = []
         wsc = [sb("wsc%d" % a, [P, H], U8) for a in range(2)]
 
         def gather(dst, win, lst):
             nc.vector.tensor_copy(dst, win[:].indirect(lst))
 
-        def cast_w(a, b):
-            half_m = P // 2
-            dst = grouped[a][:].rearrange("p (t m j) -> p m j t", t=PACK, j=PACK)[:, b * half_m : (b + 1) * half_m]
-            src = raw[a][b][:].rearrange("p j (m t) -> p m j t", t=PACK)
+        def cast_w(a):
+            dst = grouped[a][:].rearrange("p (t m j) -> p m j t", t=PACK, j=PACK)
+            src = raw[a][:].rearrange("p j (m t) -> p m j t", t=PACK)
             nc.scalar.activation(dst, src, COPY, scale=(1.0, -1.0)[a])
 
         def quant_w(a):
+            wq.append(sb("wq%d" % a, [P, H], U32))
             nc.vector.quantize_mx(out=wq[a][:].bitcast(FP8X4), scales=wsc[a][:], in_=grouped[a][:])
 
         gather(picked[:, 0, :], xs_win, offs_t[:])
-        cast_w(0, 0)
+        cast_w(0)
         gather(picked[:, 1, :], es_win, code_t[:])
-        cast_w(0, 1)
-        gather(picked[:, 2, :], vs_win, cand_t[:])
-        for q in range(4):
+        gather(picked_v[:], vs_win, cand_t[:])
+        for r in range(4):
             nc.sync.dma_start(
-                planes[32 * q : 32 * q + 4].rearrange("p a s -> p (a s)").bitcast(I32),
-                picked[4 * q : 4 * q + 4].rearrange("p a s -> p (a s)").bitcast(I32),
+                planes[r:P:32, 0:2, :].rearrange("p a s -> p (a s)").bitcast(I32),
+                picked[8 * r + 4 : P : 32].rearrange("p a s -> p (a s)").bitcast(I32),
             )
         load_words(vw_win, v_words)
+        for r in range(4):
+            nc.sync.dma_start(planes[r:P:32, 2, :].bitcast(I32), picked_v[8 * r + 4 : P : 32, :].bitcast(I32))
         gather(hg[:], h_win, cand_t[:])
-        cast_w(1, 0)
         quant_w(0)
-        cast_w(1, 1)
+        cast_w(1)
         gather(xw[:], xw_win, offs_t[:])
         quant_w(1)
-        gather(ew[:, 0:128], ew_win, code_t[:, 0:8])
-        gather(ew[:, 128:512], ew_win, code_t[:, 8:32])
+        for lo, hi in ((0, P), (P, 2 * P), (2 * P, S)):
+            gather(ew[:, lo:hi], ew_win, code_t[:, lo // 16 : hi // 16])
 
         hb = sb("hb", [P, V], F32)
         nc.sync.dma_start(hb[:], hg[0:32:4, :].unsqueeze(1).broadcast_to([8, 16, V]))
@@ -149,7 +151,7 @@ def tile_picked_yrvq_score_p_kernel(
             rr_bf.append(rb)
 
         def second(tt):
-            rq = rq_all[:, (tt % 2) * P : (tt % 2 + 1) * P]
+            rq = rq_all[:, (tt % 3) * P : (tt % 3 + 1) * P]
             rs = sb("rs%d" % tt, [P, P], U8)
             nc.vector.quantize_mx(out=rq.bitcast(FP8X4), scales=rs[:], in_=rr_bf[tt][:].rearrange("p n j -> p (n j)"))
             ob = psum.tile([P, V], F32, name="o_bank%d" % tt, tag="o%d" % tt)
@@ -158,21 +160,22 @@ def tile_picked_yrvq_score_p_kernel(
             banks.append(ob)
 
         def finish(tt):
-            res = sb("res%d" % tt, [P, V], F32, tag="rr_bf%d" % ((tt + 1) % 4))
-            nc.vector.tensor_tensor(res[:], banks[tt][:], hb[:], SUB)
-            nc.sync.dma_start(out[tt * P : (tt + 1) * P, :], res[:])
+            res = sb("res%d" % tt, [P, V], F32)
+            pieces = 2 if tt in (0, 3) else 1
+            for c in range(pieces):
+                cols = slice(c * V // pieces, (c + 1) * V // pieces)
+                nc.vector.tensor_tensor(res[:, cols], banks[tt][:, cols], hb[:, cols], SUB)
+                nc.sync.dma_start(out[tt * P : (tt + 1) * P, cols], res[:, cols])
 
-        first(0)
-        first(1)
+        for tt in range(4):
+            first(tt)
         gather(vw[:], vw_win, cand_t[:])
-        rq_all = sb("rq_all", [P, 2 * P], U32, tag="vw_win")
+        rq_all = sb("rq_all", [P, 3 * P], U32, tag="picked_v")
         second(0)
-        first(2)
         second(1)
-        finish(0)
-        first(3)
         second(2)
-        finish(1)
+        finish(0)
         second(3)
+        finish(1)
         finish(2)
         finish(3)

@@ -26,6 +26,7 @@ def tile_picked_yrvq_score_p_kernel(
     with ExitStack() as ctx:
         lists = ctx.enter_context(tc.tile_pool(name="lists", bufs=1))
         keep = ctx.enter_context(tc.tile_pool(name="keep", bufs=1))
+        turns = ctx.enter_context(tc.tile_pool(name="turns", bufs=1))
         psum = ctx.enter_context(tc.psum_pool(name="psum", bufs=1))
 
         def sb(name, shape, dtype, tag=None):
@@ -76,11 +77,10 @@ def tile_picked_yrvq_score_p_kernel(
         load_words(ew_win, e_words)
 
         picked = sb("picked", [P, 2, S], U8)
-        picked_v = sb("picked_v", [P, V], U8)
+        picked_v = turns.tile([P, V], U8, name="picked_v", align_bytes=64, offset=768)
         hg = sb("hg", [P, V], F32)
         xw = sb("xw", [P, S], U32)
         ew = sb("ew", [P, S], U32)
-        vw = sb("vw", [P, V], U32)
         grouped = [sb("grouped%d" % a, [P, PACK * H], BF16) for a in range(2)]
         wq = []
         wsc = [sb("wsc%d" % a, [P, H], U8) for a in range(2)]
@@ -117,13 +117,14 @@ def tile_picked_yrvq_score_p_kernel(
         for lo, hi in ((0, P), (P, 2 * P), (2 * P, S)):
             gather(ew[:, lo:hi], ew_win, code_t[:, lo // 16 : hi // 16])
 
-        hb = sb("hb", [P, V], F32)
-        nc.sync.dma_start(hb[:], hg[0:32:4, :].unsqueeze(1).broadcast_to([8, 16, V]))
+        hb = sb("hb", [P, V], F32, tag="grouped1")
+        for cols in (slice(0, V // 2), slice(V // 2, V)):
+            nc.scalar.dma_start(hb[:, cols], hg[0:32:4, cols].unsqueeze(1).broadcast_to([8, 16, V // 2]))
 
         rr_bf = []
         banks = []
 
-        rr_banks = [psum.tile([P, PACK, P], F32, name="rr_bank%d" % tt) for tt in range(4)]
+        rr_banks = [psum.tile([P, PACK, P], F32, name="rr_bank%d" % tt, tag="rr%d" % tt) for tt in range(4)]
 
         def x_pass(tt, j):
             cols = slice(tt * P, (tt + 1) * P)
@@ -150,32 +151,49 @@ def tile_picked_yrvq_score_p_kernel(
             nc.scalar.copy(rb[:], bank[:].rearrange("p j n -> p n j"))
             rr_bf.append(rb)
 
-        def second(tt):
-            rq = rq_all[:, (tt % 3) * P : (tt % 3 + 1) * P]
+        HV = V // 2
+        vw = []
+        rq = []
+
+        def gather_v(h, tile):
+            gather(tile[:], vw_win, cand_t[:, h * HV // 16 : (h + 1) * HV // 16])
+            vw.append(tile)
+
+        def quant_rr(tt):
+            codes = rq_all[:, (tt % 2) * P : (tt % 2 + 1) * P]
             rs = sb("rs%d" % tt, [P, P], U8)
-            nc.vector.quantize_mx(out=rq.bitcast(FP8X4), scales=rs[:], in_=rr_bf[tt][:].rearrange("p n j -> p (n j)"))
-            ob = psum.tile([P, V], F32, name="o_bank%d" % tt, tag="o%d" % tt)
-            nc.tensor.matmul_mx(out=ob[:], lhsT=rq.bitcast(FP8X4), lhsT_scale=rs[:],
-                                rhs=vw[:].bitcast(FP8X4), rhs_scale=planes[:, 2, :], start=True, stop=True)
+            nc.vector.quantize_mx(out=codes.bitcast(FP8X4), scales=rs[:], in_=rr_bf[tt][:].rearrange("p n j -> p (n j)"))
+            rq.append((codes, rs))
+
+        def second(tt, h):
+            n = 2 * tt + h
+            ob = psum.tile([P, HV], F32, name="o_bank%d" % n, tag=("o%d" % n if n < 4 else "rr%d" % (n - 4)))
+            nc.tensor.matmul_mx(out=ob[:], lhsT=rq[tt][0].bitcast(FP8X4), lhsT_scale=rq[tt][1][:],
+                                rhs=vw[h][:].bitcast(FP8X4), rhs_scale=planes[:, 2, h * HV : (h + 1) * HV], start=True, stop=True)
             banks.append(ob)
 
-        def finish(tt):
-            res = sb("res%d" % tt, [P, V], F32)
-            pieces = 2 if tt in (0, 3) else 1
-            for c in range(pieces):
-                cols = slice(c * V // pieces, (c + 1) * V // pieces)
-                nc.vector.tensor_tensor(res[:, cols], banks[tt][:, cols], hb[:, cols], SUB)
-                nc.sync.dma_start(out[tt * P : (tt + 1) * P, cols], res[:, cols])
+        def finish(tt, h):
+            n = 2 * tt + h
+            cols = slice(h * HV, (h + 1) * HV)
+            res = sb("res%d" % n, [P, HV], F32)
+            nc.vector.tensor_tensor(res[:], banks[n][:], hb[:, cols], SUB)
+            nc.sync.dma_start(out[tt * P : (tt + 1) * P, cols], res[:])
 
         for tt in range(4):
             first(tt)
-        gather(vw[:], vw_win, cand_t[:])
-        rq_all = sb("rq_all", [P, 3 * P], U32, tag="picked_v")
-        second(0)
-        second(1)
-        second(2)
-        finish(0)
-        second(3)
-        finish(1)
-        finish(2)
-        finish(3)
+        gather_v(0, sb("vw0", [P, HV], U32))
+        rq_all = turns.tile([P, 2 * P], U32, name="rq_all", align_bytes=64, offset=0)
+        quant_rr(0)
+        second(0, 0)
+        gather_v(1, turns.tile([P, HV], U32, name="vw1", align_bytes=64, offset=1024))
+        second(0, 1)
+        quant_rr(1)
+        second(1, 0)
+        second(1, 1)
+        for tt in range(4):
+            finish(tt, 0)
+            finish(tt, 1)
+            if tt < 2:
+                quant_rr(tt + 2)
+                second(tt + 2, 0)
+                second(tt + 2, 1)

@@ -138,6 +138,11 @@ def tile_picked_yrvq_score_p_kernel(
             nc.tensor.matmul_mx(out=rr_banks[tt][:, j, :], lhsT=wq[1][:, wc].bitcast(FP8X4), lhsT_scale=wsc[1][:, wc],
                                 rhs=ew[:, cols].bitcast(FP8X4), rhs_scale=planes[:, 1, cols], start=False, stop=True)
 
+        spare = psum.tile([P, V], F32, name="spare", tag="o3")
+        for turn in range(3):
+            nc.tensor.matmul_mx(out=spare[:], lhsT=wq[0][:, 0:P].bitcast(FP8X4), lhsT_scale=wsc[0][:, 0:P],
+                                rhs=wq[0][:].bitcast(FP8X4), rhs_scale=wsc[0][:], start=True, stop=True)
+
         for tt in range(4):
             x_pass(tt, 0)
 

@@ -74,7 +74,6 @@ def tile_picked_yrvq_score_p_kernel(
         nc.sync.dma_start(cand_t[:], cand)
         load_w(1, slice(0, PACK))
         load_words(xw_win, x_words)
-        load_words(ew_win, e_words)
 
         picked = sb("picked", [P, 2, S], U8)
         picked_v = turns.tile([P, V], U8, name="picked_v", align_bytes=64, offset=768)
@@ -106,13 +105,15 @@ def tile_picked_yrvq_score_p_kernel(
                 planes[r:P:32, 0:2, :].rearrange("p a s -> p (a s)").bitcast(I32),
                 picked[8 * r + 4 : P : 32].rearrange("p a s -> p (a s)").bitcast(I32),
             )
+        load_words(ew_win, e_words)
         load_words(vw_win, v_words)
         for r in range(4):
             nc.sync.dma_start(planes[r:P:32, 2, :].bitcast(I32), picked_v[8 * r + 4 : P : 32, :].bitcast(I32))
         gather(hg[:], h_win, cand_t[:])
         quant_w(0)
         cast_w(1)
-        gather(xw[:], xw_win, offs_t[:])
+        for lo, hi in ((0, P), (P, 2 * P), (2 * P, S)):
+            gather(xw[:, lo:hi], xw_win, offs_t[:, lo // 16 : hi // 16])
         quant_w(1)
         for lo, hi in ((0, P), (P, 2 * P), (2 * P, S)):
             gather(ew[:, lo:hi], ew_win, code_t[:, lo // 16 : hi // 16])
@@ -124,33 +125,35 @@ def tile_picked_yrvq_score_p_kernel(
         rr_bf = []
         banks = []
 
-        rr_banks = [psum.tile([P, PACK, P], F32, name="rr_bank%d" % tt, tag="rr%d" % tt) for tt in range(4)]
+        rr_banks = [psum.tile([P, PACK, P], F32, name="rr_bank%d" % tt, tag="rr%d" % tt) for tt in range(3)]
 
         def x_pass(tt, j):
             cols = slice(tt * P, (tt + 1) * P)
             wc = slice(j * P, (j + 1) * P)
             nc.tensor.matmul_mx(out=rr_banks[tt][:, j, :], lhsT=wq[0][:, wc].bitcast(FP8X4), lhsT_scale=wsc[0][:, wc],
-                                rhs=xw[:, cols].bitcast(FP8X4), rhs_scale=planes[:, 0, cols], start=True, stop=False)
+                                rhs=xw[:, cols].bitcast(FP8X4), rhs_scale=planes[:, 0, cols], start=(j == 0), stop=False)
 
         def e_pass(tt, j):
             cols = slice(tt * P, (tt + 1) * P)
             wc = slice(j * P, (j + 1) * P)
             nc.tensor.matmul_mx(out=rr_banks[tt][:, j, :], lhsT=wq[1][:, wc].bitcast(FP8X4), lhsT_scale=wsc[1][:, wc],
-                                rhs=ew[:, cols].bitcast(FP8X4), rhs_scale=planes[:, 1, cols], start=False, stop=True)
+                                rhs=ew[:, cols].bitcast(FP8X4), rhs_scale=planes[:, 1, cols], start=False, stop=(j == PACK - 1))
 
         spare = psum.tile([P, V], F32, name="spare", tag="o3")
-        for turn in range(3):
-            nc.tensor.matmul_mx(out=spare[:], lhsT=wq[0][:, 0:P].bitcast(FP8X4), lhsT_scale=wsc[0][:, 0:P],
-                                rhs=wq[0][:].bitcast(FP8X4), rhs_scale=wsc[0][:], start=True, stop=True)
+        nc.tensor.matmul_mx(out=spare[:], lhsT=wq[0][:, 0:P].bitcast(FP8X4), lhsT_scale=wsc[0][:, 0:P],
+                            rhs=wq[0][:].bitcast(FP8X4), rhs_scale=wsc[0][:], start=True, stop=True)
 
-        for tt in range(4):
-            x_pass(tt, 0)
+        for tt in range(3):
+            for j in range(PACK):
+                x_pass(tt, j)
 
         def first(tt):
+            if tt == 3:
+                rr_banks.append(psum.tile([P, PACK, P], F32, name="rr_bank3", tag="rr0"))
+                for j in range(PACK):
+                    x_pass(tt, j)
             bank = rr_banks[tt]
             for j in range(PACK):
-                if j > 0:
-                    x_pass(tt, j)
                 e_pass(tt, j)
             rb = sb("rr_bf%d" % tt, [P, P, PACK], BF16)
             nc.scalar.copy(rb[:], bank[:].rearrange("p j n -> p n j"))
@@ -172,7 +175,7 @@ def tile_picked_yrvq_score_p_kernel(
 
         def second(tt, h):
             n = 2 * tt + h
-            ob = psum.tile([P, HV], F32, name="o_bank%d" % n, tag=("o%d" % n if n < 4 else "rr%d" % (n - 4)))
+            ob = psum.tile([P, HV], F32, name="o_bank%d" % n, tag=("o%d" % n if n < 5 else "rr%d" % ((n - 4) % 3)))
             nc.tensor.matmul_mx(out=ob[:], lhsT=rq[tt][0].bitcast(FP8X4), lhsT_scale=rq[tt][1][:],
                                 rhs=vw[h][:].bitcast(FP8X4), rhs_scale=planes[:, 2, h * HV : (h + 1) * HV], start=True, stop=True)
             banks.append(ob)

@@ -139,10 +139,6 @@ def tile_picked_yrvq_score_p_kernel(
             nc.tensor.matmul_mx(out=rr_banks[tt][:, j, :], lhsT=wq[1][:, wc].bitcast(FP8X4), lhsT_scale=wsc[1][:, wc],
                                 rhs=ew[:, cols].bitcast(FP8X4), rhs_scale=planes[:, 1, cols], start=False, stop=(j == PACK - 1))
 
-        spare = psum.tile([P, V], F32, name="spare", tag="o3")
-        nc.tensor.matmul_mx(out=spare[:], lhsT=wq[0][:, 0:P].bitcast(FP8X4), lhsT_scale=wsc[0][:, 0:P],
-                            rhs=wq[0][:].bitcast(FP8X4), rhs_scale=wsc[0][:], start=True, stop=True)
-
         for tt in range(3):
             for j in range(PACK):
                 x_pass(tt, j)

@@ -1,6 +1,7 @@
 from contextlib import ExitStack
 
 import concourse.mybir as mybir
+from concourse.masks import make_identity
 
 F32 = mybir.dt.float32
 BF16 = mybir.dt.bfloat16
@@ -29,175 +30,182 @@ def tile_picked_yrvq_score_p_kernel(
         turns = ctx.enter_context(tc.tile_pool(name="turns", bufs=1))
         psum = ctx.enter_context(tc.psum_pool(name="psum", bufs=1))
 
-        def sb(name, shape, dtype, tag=None):
-            return keep.tile(shape, dtype, name=name, tag=tag or name, align_bytes=64)
+        def sb(name, shape, dtype):
+            return keep.tile(shape, dtype, name=name, align_bytes=64)
+
+        def at(offset, name, shape, dtype):
+            return turns.tile(shape, dtype, name=name, align_bytes=64, offset=offset)
 
         offs_t = lists.tile([P, S // 16], U16, name="offs_t")
         code_t = lists.tile([P, S // 16], U16, name="code_t")
         cand_t = lists.tile([P, V // 16], U16, name="cand_t")
 
-        xs_win = sb("xs_win", [P, T], U8)
-        es_win = sb("es_win", [P, W], U8)
-        vs_win = sb("vs_win", [P, G], U8)
-        h_win = sb("h_win", [P, G], F32)
+        VW_AT = 4 * W
+        VS_AT = VW_AT + 4 * G
+        H_AT = VS_AT + G
+        RQ_AT = H_AT + 4 * G
+        VW1_AT = RQ_AT + 8 * P
+        XS_AT = VW1_AT + 2 * V
+        HB_AT = XS_AT + T
+        xs_win = at(XS_AT, "xs_win", [P, T], U8)
+        es_win = at(VW_AT - W // 2, "es_win", [P, W], U8)
+        vs_win = at(VS_AT, "vs_win", [P, G], U8)
+        h_win = at(H_AT, "h_win", [P, G], F32)
         xw_win = sb("xw_win", [P, T], U32)
-        ew_win = sb("ew_win", [P, W], U32)
-        vw_win = sb("vw_win", [P, G], U32)
-        planes = sb("planes", [P, 3, S], U8)
         raw = [sb("raw%d" % a, [P, PACK, H], F32) for a in range(2)]
 
-        def load_scales(queue, win, scales):
-            queue.dma_start(win[4:P:8, :].bitcast(I32), scales[0].bitcast(I32))
+        def load_scales(win, scales):
+            nc.sync.dma_start(win[4:P:8, :].bitcast(I32), scales[0].bitcast(I32))
 
-        def load_words(win, words, cols=slice(None)):
-            nc.sync.dma_start(win[:, cols].bitcast(I32), words[0].rearrange("p n t -> p (n t)").bitcast(I32)[:, cols])
+        def load_words(win, words):
+            nc.sync.dma_start(win[:].bitcast(I32), words[0].rearrange("p n t -> p (n t)").bitcast(I32))
 
         def load_w(a, rows):
             w = (w1, w2)[a].rearrange("(p j) c -> p j c", j=PACK)
             nc.sync.dma_start(raw[a][:, rows, :], w[:, rows, :])
 
-        for win in (xs_win, es_win, vs_win):
-            nc.vector.memset(win[:].bitcast(I32), 0)
-        nc.vector.memset(h_win[0:64, G - 8 : G], 0.0)
-        nc.vector.memset(h_win[:, 0 : G - 8], 0.0)
-        nc.vector.memset(planes[:].rearrange("p a s -> p (a s)").bitcast(I32), 0)
-
-        nc.sync.dma_start(offs_t[:], offs)
-        load_w(0, slice(0, 1))
-        load_scales(nc.sync, xs_win, x_scales)
-        load_scales(nc.sync, es_win, e_scales)
-        nc.sync.dma_start(code_t[:], code)
-        load_scales(nc.scalar, vs_win, v_scales)
-        load_w(0, slice(1, PACK))
-        nc.scalar.dma_start(h_win[0:32:4, :], half[0:8, :])
-        nc.scalar.activation(h_win[64:P, G - 8 : G], h_win[64:P, 0:8], COPY)
-        nc.sync.dma_start(cand_t[:], cand)
-        load_w(1, slice(0, PACK))
-        load_words(xw_win, x_words)
-
-        picked = sb("picked", [P, 2, S], U8)
-        picked_v = turns.tile([P, V], U8, name="picked_v", align_bytes=64, offset=768)
-        hg = sb("hg", [P, V], F32)
-        xw = sb("xw", [P, S], U32)
-        ew = sb("ew", [P, S], U32)
-        grouped = [sb("grouped%d" % a, [P, PACK * H], BF16) for a in range(2)]
-        wq = []
-        wsc = [sb("wsc%d" % a, [P, H], U8) for a in range(2)]
-
         def gather(dst, win, lst):
             nc.vector.tensor_copy(dst, win[:].indirect(lst))
 
-        def cast_w(a):
-            dst = grouped[a][:].rearrange("p (t m j) -> p m j t", t=PACK, j=PACK)
-            src = raw[a][:].rearrange("p j (m t) -> p m j t", t=PACK)
-            nc.scalar.activation(dst, src, COPY, scale=(1.0, -1.0)[a])
+        nc.vector.memset(xs_win[:].bitcast(I32), 0)
+        nc.vector.memset(h_win[0:64, G - 8 : G], 0.0)
+        nc.vector.memset(h_win[:, 0 : G - 8], 0.0)
+        nc.vector.memset(es_win[:].bitcast(I32), 0)
+        nc.vector.memset(vs_win[:].bitcast(I32), 0)
+        nc.scalar.activation(h_win[64:P, G - 8 : G], h_win[64:P, 0:8], COPY)
 
-        def quant_w(a):
-            wq.append(sb("wq%d" % a, [P, H], U32))
-            nc.vector.quantize_mx(out=wq[a][:].bitcast(FP8X4), scales=wsc[a][:], in_=grouped[a][:])
+        nc.sync.dma_start(offs_t[:], offs)
+        load_w(0, slice(0, 1))
+        load_scales(xs_win, x_scales)
+        nc.sync.dma_start(cand_t[:], cand)
+        nc.sync.dma_start(code_t[:], code)
+        load_w(0, slice(1, 2))
+        nc.sync.dma_start(h_win[0:1, :], half[0:1, :])
+        load_scales(es_win, e_scales)
+        load_w(0, slice(2, PACK))
+        load_scales(vs_win, v_scales)
+        load_words(xw_win, x_words)
+        load_w(1, slice(0, PACK))
 
+        picked = sb("picked", [P, 2, S], U8)
+        picked_v = at(VW1_AT - V // 2, "picked_v", [P, V], U8)
         gather(picked[:, 0, :], xs_win, offs_t[:])
-        cast_w(0)
         gather(picked[:, 1, :], es_win, code_t[:])
-        gather(picked_v[:], vs_win, cand_t[:])
+        ident = at(XS_AT, "ident", [P, P], F32)
+        make_identity(nc, ident[:])
+        hg = sb("hg", [P, V], F32)
+        nc.scalar.activation(hg[:], h_win[:].indirect(cand_t[:]), COPY)
+
+        planes = sb("planes", [P, 2, S], U8)
         for r in range(4):
             nc.sync.dma_start(
-                planes[r:P:32, 0:2, :].rearrange("p a s -> p (a s)").bitcast(I32),
+                planes[r:P:32].rearrange("p a s -> p (a s)").bitcast(I32),
                 picked[8 * r + 4 : P : 32].rearrange("p a s -> p (a s)").bitcast(I32),
             )
+        ew_win = at(0, "ew_win", [P, W], U32)
+        vw_win = at(VW_AT, "vw_win", [P, G], U32)
         load_words(ew_win, e_words)
         load_words(vw_win, v_words)
+        gather(picked_v[:], vs_win, cand_t[:])
+        plane_v = sb("plane_v", [P, V], U8)
         for r in range(4):
-            nc.sync.dma_start(planes[r:P:32, 2, :].bitcast(I32), picked_v[8 * r + 4 : P : 32, :].bitcast(I32))
-        gather(hg[:], h_win, cand_t[:])
-        quant_w(0)
-        cast_w(1)
-        for lo, hi in ((0, P), (P, 2 * P), (2 * P, S)):
-            gather(xw[:, lo:hi], xw_win, offs_t[:, lo // 16 : hi // 16])
-        quant_w(1)
+            nc.sync.dma_start(plane_v[r:P:32, :].bitcast(I32), picked_v[8 * r + 4 : P : 32, :].bitcast(I32))
+
+        w1_bf = at(H_AT, "w1_bf", [P, PACK * H], BF16)
+        nc.scalar.activation(
+            w1_bf[:].rearrange("p (t m j) -> p m j t", t=PACK, j=PACK), raw[0][:].rearrange("p j (m t) -> p m j t", t=PACK), COPY
+        )
+        xw = sb("xw", [P, S], U32)
+        gather(xw[:], xw_win, offs_t[:])
+
+        turned = psum.tile([P, PACK, P], F32, name="turned", tag="o0")
+        for c in range(PACK):
+            nc.tensor.transpose(turned[:, c, :], hg[:, c * P : (c + 1) * P], ident[:])
+        h_col = sb("h_col", [P, PACK], F32)
+        nc.vector.tensor_copy(h_col[:], turned[:, :, 0])
+        spread = psum.tile([P, PACK, P], F32, name="spread", tag="o1")
+        for c in range(PACK):
+            nc.tensor.transpose(spread[:, c, :], h_col[:, c : c + 1].to_broadcast([P, P]), ident[:])
+
+        wq = [sb("wq%d" % a, [P, H], U32) for a in range(2)]
+        wsc = [sb("wsc%d" % a, [P, H], U8) for a in range(2)]
+        nc.vector.quantize_mx(out=wq[0][:].bitcast(FP8X4), scales=wsc[0][:], in_=w1_bf[:])
+
+        CUT = 96
+        w2_src = raw[1][:].rearrange("p j (m t) -> p m j t", t=PACK)
+        w2_bf = [sb("w2_bf0", [P, 2 * H], BF16), at(HB_AT, "w2_bf1", [P, 2 * H], BF16)]
+        w2_dst = [b[:].rearrange("p (t m j) -> p m j t", t=2, j=PACK) for b in w2_bf]
+        nc.vector.tensor_scalar_mul(w2_dst[0], w2_src[:, :, :, 0:2], -1.0)
+        nc.vector.tensor_scalar_mul(w2_dst[1][:, CUT:P], w2_src[:, CUT:P, :, 2:4], -1.0)
+        nc.scalar.activation(w2_dst[1][:, 0:CUT], w2_src[:, 0:CUT, :, 2:4], COPY, scale=-1.0)
+        for a in range(2):
+            cols = slice(a * 2 * P, (a + 1) * 2 * P)
+            nc.vector.quantize_mx(out=wq[1][:, cols].bitcast(FP8X4), scales=wsc[1][:, cols], in_=w2_bf[a][:])
+        hb = at(HB_AT, "hb", [P, V], F32)
+        nc.scalar.copy(hb[:], spread[:].rearrange("p c n -> p (c n)"))
+        ew = sb("ew", [P, S], U32)
         for lo, hi in ((0, P), (P, 2 * P), (2 * P, S)):
             gather(ew[:, lo:hi], ew_win, code_t[:, lo // 16 : hi // 16])
 
-        hb = sb("hb", [P, V], F32, tag="grouped1")
-        for cols in (slice(0, V // 2), slice(V // 2, V)):
-            nc.scalar.dma_start(hb[:, cols], hg[0:32:4, cols].unsqueeze(1).broadcast_to([8, 16, V // 2]))
+        rr_banks = [psum.tile([P, PACK, P], F32, name="rr_bank%d" % tt, tag="rr%d" % tt) for tt in range(4)]
 
+        def passes(a, tt, first):
+            cols = slice(tt * P, (tt + 1) * P)
+            words = (xw, ew)[a][:, cols]
+            for j in range(PACK):
+                wc = slice(j * P, (j + 1) * P)
+                nc.tensor.matmul_mx(out=rr_banks[tt][:, j, :], lhsT=wq[a][:, wc].bitcast(FP8X4), lhsT_scale=wsc[a][:, wc],
+                                    rhs=words.bitcast(FP8X4), rhs_scale=planes[:, a, cols],
+                                    start=(first and j == 0), stop=(not first and j == PACK - 1))
+
+        for tt in range(2):
+            passes(0, tt, True)
         rr_bf = []
-        banks = []
-
-        rr_banks = [psum.tile([P, PACK, P], F32, name="rr_bank%d" % tt, tag="rr%d" % tt) for tt in range(3)]
-
-        def x_pass(tt, j):
-            cols = slice(tt * P, (tt + 1) * P)
-            wc = slice(j * P, (j + 1) * P)
-            nc.tensor.matmul_mx(out=rr_banks[tt][:, j, :], lhsT=wq[0][:, wc].bitcast(FP8X4), lhsT_scale=wsc[0][:, wc],
-                                rhs=xw[:, cols].bitcast(FP8X4), rhs_scale=planes[:, 0, cols], start=(j == 0), stop=False)
-
-        def e_pass(tt, j):
-            cols = slice(tt * P, (tt + 1) * P)
-            wc = slice(j * P, (j + 1) * P)
-            nc.tensor.matmul_mx(out=rr_banks[tt][:, j, :], lhsT=wq[1][:, wc].bitcast(FP8X4), lhsT_scale=wsc[1][:, wc],
-                                rhs=ew[:, cols].bitcast(FP8X4), rhs_scale=planes[:, 1, cols], start=False, stop=(j == PACK - 1))
-
-        for tt in range(3):
-            for j in range(PACK):
-                x_pass(tt, j)
-
-        def first(tt):
-            if tt == 3:
-                rr_banks.append(psum.tile([P, PACK, P], F32, name="rr_bank3", tag="rr0"))
-                for j in range(PACK):
-                    x_pass(tt, j)
-            bank = rr_banks[tt]
-            for j in range(PACK):
-                e_pass(tt, j)
+        for tt in range(4):
+            passes(1, tt, tt >= 2)
+            if tt >= 2:
+                passes(0, tt, False)
             rb = sb("rr_bf%d" % tt, [P, P, PACK], BF16)
-            nc.scalar.copy(rb[:], bank[:].rearrange("p j n -> p n j"))
+            nc.scalar.copy(rb[:], rr_banks[tt][:].rearrange("p j n -> p n j"))
             rr_bf.append(rb)
 
         HV = V // 2
         vw = []
-        rq = []
+        rq, rs = [], []
+        res = [sb("res%d" % tt, [P, V], F32) for tt in range(4)]
 
-        def gather_v(h, tile):
-            gather(tile[:], vw_win, cand_t[:, h * HV // 16 : (h + 1) * HV // 16])
-            vw.append(tile)
+        def gather_v(h):
+            vw.append(at(VW1_AT, "vw1", [P, HV], U32) if h else sb("vw0", [P, HV], U32))
+            gather(vw[h][:], vw_win, cand_t[:, h * HV // 16 : (h + 1) * HV // 16])
 
         def quant_rr(tt):
-            codes = rq_all[:, (tt % 2) * P : (tt % 2 + 1) * P]
-            rs = sb("rs%d" % tt, [P, P], U8)
-            nc.vector.quantize_mx(out=codes.bitcast(FP8X4), scales=rs[:], in_=rr_bf[tt][:].rearrange("p n j -> p (n j)"))
-            rq.append((codes, rs))
+            rq.append(rq_pair[:, (tt % 2) * P : (tt % 2 + 1) * P])
+            rs.append(sb("rs%d" % tt, [P, P], U8))
+            nc.vector.quantize_mx(out=rq[tt].bitcast(FP8X4), scales=rs[tt][:], in_=rr_bf[tt][:].rearrange("p n j -> p (n j)"))
 
-        def second(tt, h):
-            n = 2 * tt + h
-            ob = psum.tile([P, HV], F32, name="o_bank%d" % n, tag=("o%d" % n if n < 5 else "rr%d" % ((n - 4) % 3)))
-            nc.tensor.matmul_mx(out=ob[:], lhsT=rq[tt][0].bitcast(FP8X4), lhsT_scale=rq[tt][1][:],
-                                rhs=vw[h][:].bitcast(FP8X4), rhs_scale=planes[:, 2, h * HV : (h + 1) * HV], start=True, stop=True)
-            banks.append(ob)
+        def product(tt, cols, tag):
+            ob = psum.tile([P, cols.stop - cols.start], F32, name="o_bank%d_%d" % (tt, cols.start), tag=tag)
+            for h in range(cols.start // HV, cols.stop // HV):
+                nc.tensor.matmul_mx(out=ob[:, h * HV - cols.start : (h + 1) * HV - cols.start], lhsT=rq[tt].bitcast(FP8X4), lhsT_scale=rs[tt][:],
+                                    rhs=vw[h][:].bitcast(FP8X4), rhs_scale=plane_v[:, h * HV : (h + 1) * HV], start=True, stop=True)
+            return ob
 
-        def finish(tt, h):
-            n = 2 * tt + h
-            cols = slice(h * HV, (h + 1) * HV)
-            res = sb("res%d" % n, [P, HV], F32)
-            nc.vector.tensor_tensor(res[:], banks[n][:], hb[:, cols], SUB)
-            nc.sync.dma_start(out[tt * P : (tt + 1) * P, cols], res[:])
+        def finish(tt, cols, ob):
+            nc.vector.tensor_tensor(res[tt][:, cols], ob[:], hb[:, cols], SUB)
+            nc.sync.dma_start(out[tt * P : (tt + 1) * P, cols], res[tt][:, cols])
 
-        for tt in range(4):
-            first(tt)
-        gather_v(0, sb("vw0", [P, HV], U32))
-        rq_all = turns.tile([P, 2 * P], U32, name="rq_all", align_bytes=64, offset=0)
+        lo, hi = slice(0, HV), slice(HV, V)
+        tags = ["o0", "o1", "o2", "o3", "rr0", "rr1", "rr2", "rr3"]
+        gather_v(0)
+        rq_pair = at(RQ_AT, "rq_pair", [P, 2 * P], U32)
         quant_rr(0)
-        second(0, 0)
-        gather_v(1, turns.tile([P, HV], U32, name="vw1", align_bytes=64, offset=1024))
-        second(0, 1)
+        banks = [product(0, lo, tags[0])]
+        gather_v(1)
         quant_rr(1)
-        second(1, 0)
-        second(1, 1)
+        banks += [product(0, hi, tags[1]), product(1, lo, tags[2]), product(1, hi, tags[3])]
         for tt in range(4):
-            finish(tt, 0)
-            finish(tt, 1)
+            finish(tt, lo, banks[2 * tt])
+            finish(tt, hi, banks[2 * tt + 1])
             if tt < 2:
                 quant_rr(tt + 2)
-                second(tt + 2, 0)
-                second(tt + 2, 1)
+                banks += [product(tt + 2, lo, tags[2 * tt + 4]), product(tt + 2, hi, tags[2 * tt + 5])]

@@ -31,117 +31,126 @@ def tile_picked_yrvq_score_p_kernel(
         psum = ctx.enter_context(tc.psum_pool(name="psum", bufs=1))
 
         def sb(name, shape, dtype):
-            return keep.tile(shape, dtype, name=name, align_bytes=64)
+            return keep.tile(shape, dtype, name=name, align_bytes=256)
 
         def at(offset, name, shape, dtype):
-            return turns.tile(shape, dtype, name=name, align_bytes=64, offset=offset)
+            return turns.tile(shape, dtype, name=name, align_bytes=256, offset=offset)
 
         offs_t = lists.tile([P, S // 16], U16, name="offs_t")
         code_t = lists.tile([P, S // 16], U16, name="code_t")
         cand_t = lists.tile([P, V // 16], U16, name="cand_t")
 
-        VW_AT = 4 * W
-        VS_AT = VW_AT + 4 * G
-        H_AT = VS_AT + G
-        RQ_AT = H_AT + 4 * G
-        VW1_AT = RQ_AT + 8 * P
-        XS_AT = VW1_AT + 2 * V
-        HB_AT = XS_AT + T
-        xs_win = at(XS_AT, "xs_win", [P, T], U8)
-        es_win = at(VW_AT - W // 2, "es_win", [P, W], U8)
-        vs_win = at(VS_AT, "vs_win", [P, G], U8)
+        LAP = 256
+        HGA_AT = 4 * W - LAP
+        VW_AT = HGA_AT + 2 * V - LAP
+        W2B_AT = VW_AT + 4 * G
+        HGB_AT = W2B_AT + 2 * PACK * H - LAP
+        XG_AT = HGB_AT + 2 * V - LAP
+        H_AT = XG_AT + 4 * S
+        W2_AT = H_AT + 4 * G
+        RQ_AT = W2_AT + 4 * PACK * H
+        PV_AT = RQ_AT + 3 * 4 * P - LAP
+        VW1_AT = PV_AT + V - LAP
+        xs_win = sb("xs_win", [P, T + 4], U8)
+        es_win = sb("es_win", [P, W + 4], U8)
+        vs_win = sb("vs_win", [P, G], U8)
         h_win = at(H_AT, "h_win", [P, G], F32)
         xw_win = sb("xw_win", [P, T], U32)
-        raw = [sb("raw%d" % a, [P, PACK, H], F32) for a in range(2)]
+        raw = [sb("raw0", [P, PACK, H], F32), at(W2_AT, "raw1", [P, PACK, H], F32)]
+        ROW = P - 1
+        ROWS = P - 16
 
         def load_scales(win, scales):
-            nc.sync.dma_start(win[4:P:8, :].bitcast(I32), scales[0].bitcast(I32))
+            nc.scalar.dma_start(win[ROWS:P, 0 : scales.shape[2]].bitcast(I32), scales[0].bitcast(I32))
 
         def load_words(win, words):
             nc.sync.dma_start(win[:].bitcast(I32), words[0].rearrange("p n t -> p (n t)").bitcast(I32))
 
-        def load_w(a, rows):
-            w = (w1, w2)[a].rearrange("(p j) c -> p j c", j=PACK)
-            nc.sync.dma_start(raw[a][:, rows, :], w[:, rows, :])
+        def load_w(a):
+            nc.sync.dma_start(raw[a][:], (w1, w2)[a].rearrange("(p j) c -> p j c", j=PACK))
 
         def gather(dst, win, lst):
             nc.vector.tensor_copy(dst, win[:].indirect(lst))
 
-        nc.vector.memset(xs_win[:].bitcast(I32), 0)
-        nc.vector.memset(h_win[0:64, G - 8 : G], 0.0)
-        nc.vector.memset(h_win[:, 0 : G - 8], 0.0)
-        nc.vector.memset(es_win[:].bitcast(I32), 0)
-        nc.vector.memset(vs_win[:].bitcast(I32), 0)
-        nc.scalar.activation(h_win[64:P, G - 8 : G], h_win[64:P, 0:8], COPY)
+        POOL_COLS = 768
+        CORNER = G - 7
+        nc.vector.memset(xs_win[0:ROWS, :].bitcast(I32), 0)
+        nc.vector.memset(es_win[0:ROWS, :].bitcast(I32), 0)
+        nc.vector.memset(h_win[0:ROW, POOL_COLS:CORNER], 0.0)
+        nc.gpsimd.memset(vs_win[0:ROWS, :].bitcast(I32), 0)
+        ident = sb("ident", [P, P], F32)
+        make_identity(nc, ident[:])
+        nc.gpsimd.memset(h_win[0:ROW, 0:POOL_COLS], 0.0)
 
         nc.sync.dma_start(offs_t[:], offs)
-        load_w(0, slice(0, 1))
         load_scales(xs_win, x_scales)
-        nc.sync.dma_start(cand_t[:], cand)
         nc.sync.dma_start(code_t[:], code)
-        load_w(0, slice(1, 2))
-        nc.sync.dma_start(h_win[0:1, :], half[0:1, :])
+        nc.scalar.dma_start(h_win[ROW:P, :], half[0:1, :])
+        nc.sync.dma_start(cand_t[:], cand)
         load_scales(es_win, e_scales)
-        load_w(0, slice(2, PACK))
         load_scales(vs_win, v_scales)
+        load_w(0)
         load_words(xw_win, x_words)
-        load_w(1, slice(0, PACK))
+        load_w(1)
+        nc.scalar.activation(h_win[0:ROW, CORNER:G], h_win[0:ROW, POOL_COLS : POOL_COLS + G - CORNER], COPY)
 
         picked = sb("picked", [P, 2, S], U8)
-        picked_v = at(VW1_AT - V // 2, "picked_v", [P, V], U8)
+        picked_v = at(PV_AT, "picked_v", [P, V], U8)
         gather(picked[:, 0, :], xs_win, offs_t[:])
         gather(picked[:, 1, :], es_win, code_t[:])
-        ident = at(XS_AT, "ident", [P, P], F32)
-        make_identity(nc, ident[:])
-        hg = sb("hg", [P, V], F32)
-        nc.scalar.activation(hg[:], h_win[:].indirect(cand_t[:]), COPY)
+        gather(picked_v[:], vs_win, cand_t[:])
+        HV = V // 2
+        hg = [at(HGA_AT, "hg0", [P, HV], F32), at(HGB_AT, "hg1", [P, HV], F32)]
+        for h in range(2):
+            nc.scalar.activation(hg[h][:], h_win[:].indirect(cand_t[:, h * HV // 16 : (h + 1) * HV // 16]), COPY)
 
         planes = sb("planes", [P, 2, S], U8)
         for r in range(4):
             nc.sync.dma_start(
                 planes[r:P:32].rearrange("p a s -> p (a s)").bitcast(I32),
-                picked[8 * r + 4 : P : 32].rearrange("p a s -> p (a s)").bitcast(I32),
+                picked[ROWS + r : P : 4].rearrange("p a s -> p (a s)").bitcast(I32),
             )
         ew_win = at(0, "ew_win", [P, W], U32)
         vw_win = at(VW_AT, "vw_win", [P, G], U32)
         load_words(ew_win, e_words)
         load_words(vw_win, v_words)
-        gather(picked_v[:], vs_win, cand_t[:])
         plane_v = sb("plane_v", [P, V], U8)
         for r in range(4):
-            nc.sync.dma_start(plane_v[r:P:32, :].bitcast(I32), picked_v[8 * r + 4 : P : 32, :].bitcast(I32))
-
-        w1_bf = at(H_AT, "w1_bf", [P, PACK * H], BF16)
-        nc.scalar.activation(
-            w1_bf[:].rearrange("p (t m j) -> p m j t", t=PACK, j=PACK), raw[0][:].rearrange("p j (m t) -> p m j t", t=PACK), COPY
-        )
-        xw = sb("xw", [P, S], U32)
-        gather(xw[:], xw_win, offs_t[:])
+            nc.sync.dma_start(plane_v[r:P:32, :].bitcast(I32), picked_v[ROWS + r : P : 4, :].bitcast(I32))
 
         turned = psum.tile([P, PACK, P], F32, name="turned", tag="o0")
         for c in range(PACK):
-            nc.tensor.transpose(turned[:, c, :], hg[:, c * P : (c + 1) * P], ident[:])
+            nc.tensor.transpose(turned[:, c, :], hg[c // 2][:, (c % 2) * P : (c % 2 + 1) * P], ident[:])
         h_col = sb("h_col", [P, PACK], F32)
-        nc.vector.tensor_copy(h_col[:], turned[:, :, 0])
+        nc.vector.tensor_copy(h_col[:], turned[:, :, ROW])
         spread = psum.tile([P, PACK, P], F32, name="spread", tag="o1")
         for c in range(PACK):
             nc.tensor.transpose(spread[:, c, :], h_col[:, c : c + 1].to_broadcast([P, P]), ident[:])
 
+        w_bf = [at(H_AT, "w1_bf", [P, PACK * H], BF16), at(W2B_AT, "w2_bf", [P, PACK * H], BF16)]
         wq = [sb("wq%d" % a, [P, H], U32) for a in range(2)]
-        wsc = [sb("wsc%d" % a, [P, H], U8) for a in range(2)]
-        nc.vector.quantize_mx(out=wq[0][:].bitcast(FP8X4), scales=wsc[0][:], in_=w1_bf[:])
+        wsc = [at(HGB_AT + LAP, "wsc0", [P, H], U8), sb("wsc1", [P, H], U8)]
+        SHARE = (0, 72)
 
-        CUT = 96
-        w2_src = raw[1][:].rearrange("p j (m t) -> p m j t", t=PACK)
-        w2_bf = [sb("w2_bf0", [P, 2 * H], BF16), at(HB_AT, "w2_bf1", [P, 2 * H], BF16)]
-        w2_dst = [b[:].rearrange("p (t m j) -> p m j t", t=2, j=PACK) for b in w2_bf]
-        nc.vector.tensor_scalar_mul(w2_dst[0], w2_src[:, :, :, 0:2], -1.0)
-        nc.vector.tensor_scalar_mul(w2_dst[1][:, CUT:P], w2_src[:, CUT:P, :, 2:4], -1.0)
-        nc.scalar.activation(w2_dst[1][:, 0:CUT], w2_src[:, 0:CUT, :, 2:4], COPY, scale=-1.0)
-        for a in range(2):
-            cols = slice(a * 2 * P, (a + 1) * 2 * P)
-            nc.vector.quantize_mx(out=wq[1][:, cols].bitcast(FP8X4), scales=wsc[1][:, cols], in_=w2_bf[a][:])
-        hb = at(HB_AT, "hb", [P, V], F32)
+        def round_w(a):
+            cut = P - SHARE[a]
+            src = raw[a][:].rearrange("p j (m t) -> p m j t", t=PACK)
+            dst = w_bf[a][:].rearrange("p (t m j) -> p m j t", t=PACK, j=PACK)
+            nc.scalar.activation(dst[:, 0:cut], src[:, 0:cut], COPY, scale=(1.0, -1.0)[a])
+            if SHARE[a]:
+                for u in (0, 2):
+                    nc.vector.tensor_scalar_mul(dst[:, cut:P, :, u : u + 2], src[:, cut:P, :, u : u + 2], (1.0, -1.0)[a])
+
+        def quant_w(a):
+            nc.vector.quantize_mx(out=wq[a][:].bitcast(FP8X4), scales=wsc[a][:], in_=w_bf[a][:])
+
+        xw = at(XG_AT, "xw", [P, S], U32)
+        gather(xw[:], xw_win, offs_t[:])
+        round_w(0)
+        quant_w(0)
+        round_w(1)
+        quant_w(1)
+        hb = at(W2_AT, "hb", [P, V], F32)
         nc.scalar.copy(hb[:], spread[:].rearrange("p c n -> p (c n)"))
         ew = sb("ew", [P, S], U32)
         for lo, hi in ((0, P), (P, 2 * P), (2 * P, S)):
@@ -158,36 +167,35 @@ def tile_picked_yrvq_score_p_kernel(
                                     rhs=words.bitcast(FP8X4), rhs_scale=planes[:, a, cols],
                                     start=(first and j == 0), stop=(not first and j == PACK - 1))
 
-        for tt in range(2):
+        AHEAD = 3
+        for tt in range(AHEAD):
             passes(0, tt, True)
         rr_bf = []
         for tt in range(4):
-            passes(1, tt, tt >= 2)
-            if tt >= 2:
+            passes(1, tt, tt >= AHEAD)
+            if tt >= AHEAD:
                 passes(0, tt, False)
             rb = sb("rr_bf%d" % tt, [P, P, PACK], BF16)
             nc.scalar.copy(rb[:], rr_banks[tt][:].rearrange("p j n -> p n j"))
             rr_bf.append(rb)
 
-        HV = V // 2
-        vw = []
+        vw = [sb("vw0", [P, HV], U32), at(VW1_AT, "vw1", [P, HV], U32)]
+        slots = at(RQ_AT, "slots", [P, 3 * P], U32)
         rq, rs = [], []
         res = [sb("res%d" % tt, [P, V], F32) for tt in range(4)]
 
         def gather_v(h):
-            vw.append(at(VW1_AT, "vw1", [P, HV], U32) if h else sb("vw0", [P, HV], U32))
             gather(vw[h][:], vw_win, cand_t[:, h * HV // 16 : (h + 1) * HV // 16])
 
         def quant_rr(tt):
-            rq.append(rq_pair[:, (tt % 2) * P : (tt % 2 + 1) * P])
+            rq.append(slots[:, (tt % 3) * P : (tt % 3 + 1) * P])
             rs.append(sb("rs%d" % tt, [P, P], U8))
             nc.vector.quantize_mx(out=rq[tt].bitcast(FP8X4), scales=rs[tt][:], in_=rr_bf[tt][:].rearrange("p n j -> p (n j)"))
 
         def product(tt, cols, tag):
-            ob = psum.tile([P, cols.stop - cols.start], F32, name="o_bank%d_%d" % (tt, cols.start), tag=tag)
-            for h in range(cols.start // HV, cols.stop // HV):
-                nc.tensor.matmul_mx(out=ob[:, h * HV - cols.start : (h + 1) * HV - cols.start], lhsT=rq[tt].bitcast(FP8X4), lhsT_scale=rs[tt][:],
-                                    rhs=vw[h][:].bitcast(FP8X4), rhs_scale=plane_v[:, h * HV : (h + 1) * HV], start=True, stop=True)
+            ob = psum.tile([P, HV], F32, name="o_bank%d_%d" % (tt, cols.start), tag=tag)
+            nc.tensor.matmul_mx(out=ob[:], lhsT=rq[tt].bitcast(FP8X4), lhsT_scale=rs[tt][:],
+                                rhs=vw[cols.start // HV][:].bitcast(FP8X4), rhs_scale=plane_v[:, cols], start=True, stop=True)
             return ob
 
         def finish(tt, cols, ob):
@@ -195,17 +203,26 @@ def tile_picked_yrvq_score_p_kernel(
             nc.sync.dma_start(out[tt * P : (tt + 1) * P, cols], res[tt][:, cols])
 
         lo, hi = slice(0, HV), slice(HV, V)
-        tags = ["o0", "o1", "o2", "o3", "rr0", "rr1", "rr2", "rr3"]
+        def finish_aside(tt, cols, ob):
+            nc.scalar.copy(plain[:, cols], ob[:])
+            nc.gpsimd.tensor_tensor(res[tt][:, cols], plain[:, cols], hb[:, cols], SUB)
+            nc.scalar.dma_start(out[tt * P : (tt + 1) * P, cols], res[tt][:, cols])
+
+        plain = sb("plain", [P, HV], F32)
         gather_v(0)
-        rq_pair = at(RQ_AT, "rq_pair", [P, 2 * P], U32)
         quant_rr(0)
-        banks = [product(0, lo, tags[0])]
         gather_v(1)
         quant_rr(1)
-        banks += [product(0, hi, tags[1]), product(1, lo, tags[2]), product(1, hi, tags[3])]
-        for tt in range(4):
-            finish(tt, lo, banks[2 * tt])
-            finish(tt, hi, banks[2 * tt + 1])
-            if tt < 2:
-                quant_rr(tt + 2)
-                banks += [product(tt + 2, lo, tags[2 * tt + 4]), product(tt + 2, hi, tags[2 * tt + 5])]
+        b0 = [product(0, lo, "o0"), product(0, hi, "o1")]
+        b1 = [product(1, lo, "o2"), product(1, hi, "o3")]
+        finish(0, lo, b0[0])
+        quant_rr(2)
+        b2 = [product(2, lo, "rr0"), product(2, hi, "rr1")]
+        finish(0, hi, b0[1])
+        quant_rr(3)
+        b3 = [product(3, lo, "rr2"), product(3, hi, "rr3")]
+        finish_aside(1, lo, b1[0])
+        finish(1, hi, b1[1])
+        for tt, b in ((2, b2), (3, b3)):
+            finish(tt, lo, b[0])
+            finish(tt, hi, b[1])

@@ -130,26 +130,22 @@ def tile_picked_yrvq_score_p_kernel(
         w_bf = [at(H_AT, "w1_bf", [P, PACK * H], BF16), at(W2B_AT, "w2_bf", [P, PACK * H], BF16)]
         wq = [sb("wq%d" % a, [P, H], U32) for a in range(2)]
         wsc = [at(HGB_AT + LAP, "wsc0", [P, H], U8), sb("wsc1", [P, H], U8)]
-        SHARE = (0, 72)
+        src = [r[:].rearrange("p j (m t) -> p m j t", t=PACK) for r in raw]
+        dst = [b[:].rearrange("p (t m j) -> p m j t", t=PACK, j=PACK) for b in w_bf]
+        CUT = 96
 
-        def round_w(a):
-            cut = P - SHARE[a]
-            src = raw[a][:].rearrange("p j (m t) -> p m j t", t=PACK)
-            dst = w_bf[a][:].rearrange("p (t m j) -> p m j t", t=PACK, j=PACK)
-            nc.scalar.activation(dst[:, 0:cut], src[:, 0:cut], COPY, scale=(1.0, -1.0)[a])
-            if SHARE[a]:
-                for u in (0, 2):
-                    nc.vector.tensor_scalar_mul(dst[:, cut:P, :, u : u + 2], src[:, cut:P, :, u : u + 2], (1.0, -1.0)[a])
-
-        def quant_w(a):
-            nc.vector.quantize_mx(out=wq[a][:].bitcast(FP8X4), scales=wsc[a][:], in_=w_bf[a][:])
+        def quant_w(a, lo, hi):
+            nc.vector.quantize_mx(out=wq[a][:, lo:hi].bitcast(FP8X4), scales=wsc[a][:, lo:hi], in_=w_bf[a][:, PACK * lo : PACK * hi])
 
         xw = at(XG_AT, "xw", [P, S], U32)
         gather(xw[:], xw_win, offs_t[:])
-        round_w(0)
-        quant_w(0)
-        round_w(1)
-        quant_w(1)
+        nc.scalar.activation(dst[0], src[0], COPY)
+        quant_w(0, 0, H)
+        nc.vector.tensor_scalar_mul(dst[1][:, :, :, 0:2], src[1][:, :, :, 0:2], -1.0)
+        nc.vector.tensor_scalar_mul(dst[1][:, CUT:P, :, 2:4], src[1][:, CUT:P, :, 2:4], -1.0)
+        nc.scalar.activation(dst[1][:, 0:CUT, :, 2:4], src[1][:, 0:CUT, :, 2:4], COPY, scale=-1.0)
+        quant_w(1, 0, H // 2)
+        quant_w(1, H // 2, H)
         hb = at(W2_AT, "hb", [P, V], F32)
         nc.scalar.copy(hb[:], spread[:].rearrange("p c n -> p (c n)"))
         ew = sb("ew", [P, S], U32)

@@ -149,7 +149,7 @@ def tile_picked_yrvq_score_p_kernel(
         hb = at(W2_AT, "hb", [P, V], F32)
         nc.scalar.copy(hb[:], spread[:].rearrange("p c n -> p (c n)"))
         ew = sb("ew", [P, S], U32)
-        for lo, hi in ((0, P), (P, 2 * P), (2 * P, S)):
+        for lo, hi in ((0, P), (P, 2 * P), (2 * P, 3 * P), (3 * P, S)):
             gather(ew[:, lo:hi], ew_win, code_t[:, lo // 16 : hi // 16])
 
         rr_banks = [psum.tile([P, PACK, P], F32, name="rr_bank%d" % tt, tag="rr%d" % tt) for tt in range(4)]
@@ -163,7 +163,7 @@ def tile_picked_yrvq_score_p_kernel(
                                     rhs=words.bitcast(FP8X4), rhs_scale=planes[:, a, cols],
                                     start=(first and j == 0), stop=(not first and j == PACK - 1))
 
-        AHEAD = 3
+        AHEAD = 2
         for tt in range(AHEAD):
             passes(0, tt, True)
         rr_bf = []

from contextlib import ExitStack

import concourse.mybir as mybir
from concourse.masks import make_identity

F32 = mybir.dt.float32
BF16 = mybir.dt.bfloat16
I32 = mybir.dt.int32
U32 = mybir.dt.uint32
U16 = mybir.dt.uint16
U8 = mybir.dt.uint8
FP8X4 = mybir.dt.float8_e4m3fn_x4
COPY = mybir.ActivationFunctionType.Copy
SUB = mybir.AluOpType.subtract

P = 128
PACK = 4
K, T, S, H, V, W, G = 512, 1024, 512, 512, 512, 1024, 2048
FLOPS = 2 * (2 * K * H * S + H * S * V)
BYTES = K * (T + W + G) + (K // 32) * (T + W + G) + 2 * 4 * K * H + 4 * G + 3 * 2 * P * 32 + 4 * S * V


def tile_picked_yrvq_score_p_kernel(
    tc, x_words, x_scales, e_words, e_scales, w1, w2, v_words, v_scales, half, offs, code, cand, out
):
    nc = tc.nc
    with ExitStack() as ctx:
        lists = ctx.enter_context(tc.tile_pool(name="lists", bufs=1))
        keep = ctx.enter_context(tc.tile_pool(name="keep", bufs=1))
        turns = ctx.enter_context(tc.tile_pool(name="turns", bufs=1))
        psum = ctx.enter_context(tc.psum_pool(name="psum", bufs=1))

        def sb(name, shape, dtype):
            return keep.tile(shape, dtype, name=name, align_bytes=256)

        def at(offset, name, shape, dtype):
            return turns.tile(shape, dtype, name=name, align_bytes=256, offset=offset)

        offs_t = lists.tile([P, S // 16], U16, name="offs_t")
        code_t = lists.tile([P, S // 16], U16, name="code_t")
        cand_t = lists.tile([P, V // 16], U16, name="cand_t")

        LAP = 256
        HGA_AT = 4 * W - LAP
        VW_AT = HGA_AT + 2 * V - LAP
        W2B_AT = VW_AT + 4 * G
        HGB_AT = W2B_AT + 2 * PACK * H - LAP
        XG_AT = HGB_AT + 2 * V - LAP
        H_AT = XG_AT + 4 * S
        W2_AT = H_AT + 4 * G
        RQ_AT = W2_AT + 4 * PACK * H
        PV_AT = RQ_AT + 3 * 4 * P - LAP
        VW1_AT = PV_AT + V - LAP
        xs_win = sb("xs_win", [P, T + 4], U8)
        es_win = sb("es_win", [P, W + 4], U8)
        vs_win = sb("vs_win", [P, G], U8)
        h_win = at(H_AT, "h_win", [P, G], F32)
        xw_win = sb("xw_win", [P, T], U32)
        raw = [sb("raw0", [P, PACK, H], F32), at(W2_AT, "raw1", [P, PACK, H], F32)]
        ROW = P - 1
        ROWS = P - 16

        def load_scales(win, scales):
            nc.scalar.dma_start(win[ROWS:P, 0 : scales.shape[2]].bitcast(I32), scales[0].bitcast(I32))

        def load_words(win, words):
            nc.sync.dma_start(win[:].bitcast(I32), words[0].rearrange("p n t -> p (n t)").bitcast(I32))

        def load_w(a):
            nc.sync.dma_start(raw[a][:], (w1, w2)[a].rearrange("(p j) c -> p j c", j=PACK))

        def gather(dst, win, lst):
            nc.vector.tensor_copy(dst, win[:].indirect(lst))

        POOL_COLS = 768
        CORNER = G - 7
        nc.vector.memset(xs_win[0:ROWS, :].bitcast(I32), 0)
        nc.vector.memset(es_win[0:ROWS, :].bitcast(I32), 0)
        nc.vector.memset(h_win[0:ROW, POOL_COLS:CORNER], 0.0)
        nc.gpsimd.memset(vs_win[0:ROWS, :].bitcast(I32), 0)
        ident = sb("ident", [P, P], F32)
        make_identity(nc, ident[:])
        nc.gpsimd.memset(h_win[0:ROW, 0:POOL_COLS], 0.0)

        nc.sync.dma_start(offs_t[:], offs)
        load_scales(xs_win, x_scales)
        nc.sync.dma_start(code_t[:], code)
        nc.scalar.dma_start(h_win[ROW:P, :], half[0:1, :])
        nc.sync.dma_start(cand_t[:], cand)
        load_scales(es_win, e_scales)
        load_scales(vs_win, v_scales)
        load_w(0)
        load_words(xw_win, x_words)
        load_w(1)
        nc.scalar.activation(h_win[0:ROW, CORNER:G], h_win[0:ROW, POOL_COLS : POOL_COLS + G - CORNER], COPY)

        picked = sb("picked", [P, 2, S], U8)
        picked_v = at(PV_AT, "picked_v", [P, V], U8)
        gather(picked[:, 0, :], xs_win, offs_t[:])
        gather(picked[:, 1, :], es_win, code_t[:])
        gather(picked_v[:], vs_win, cand_t[:])
        HV = V // 2
        hg = [at(HGA_AT, "hg0", [P, HV], F32), at(HGB_AT, "hg1", [P, HV], F32)]
        for h in range(2):
            nc.scalar.activation(hg[h][:], h_win[:].indirect(cand_t[:, h * HV // 16 : (h + 1) * HV // 16]), COPY)

        planes = sb("planes", [P, 2, S], U8)
        for r in range(4):
            nc.sync.dma_start(
                planes[r:P:32].rearrange("p a s -> p (a s)").bitcast(I32),
                picked[ROWS + r : P : 4].rearrange("p a s -> p (a s)").bitcast(I32),
            )
        ew_win = at(0, "ew_win", [P, W], U32)
        vw_win = at(VW_AT, "vw_win", [P, G], U32)
        load_words(ew_win, e_words)
        load_words(vw_win, v_words)
        plane_v = sb("plane_v", [P, V], U8)
        for r in range(4):
            nc.sync.dma_start(plane_v[r:P:32, :].bitcast(I32), picked_v[ROWS + r : P : 4, :].bitcast(I32))

        turned = psum.tile([P, PACK, P], F32, name="turned", tag="o0")
        for c in range(PACK):
            nc.tensor.transpose(turned[:, c, :], hg[c // 2][:, (c % 2) * P : (c % 2 + 1) * P], ident[:])
        h_col = sb("h_col", [P, PACK], F32)
        nc.vector.tensor_copy(h_col[:], turned[:, :, ROW])
        spread = psum.tile([P, PACK, P], F32, name="spread", tag="o1")
        for c in range(PACK):
            nc.tensor.transpose(spread[:, c, :], h_col[:, c : c + 1].to_broadcast([P, P]), ident[:])

        w_bf = [at(H_AT, "w1_bf", [P, PACK * H], BF16), at(W2B_AT, "w2_bf", [P, PACK * H], BF16)]
        wq = [sb("wq%d" % a, [P, H], U32) for a in range(2)]
        wsc = [at(HGB_AT + LAP, "wsc0", [P, H], U8), sb("wsc1", [P, H], U8)]
        src = [r[:].rearrange("p j (m t) -> p m j t", t=PACK) for r in raw]
        dst = [b[:].rearrange("p (t m j) -> p m j t", t=PACK, j=PACK) for b in w_bf]
        CUT = 96

        def quant_w(a, lo, hi):
            nc.vector.quantize_mx(out=wq[a][:, lo:hi].bitcast(FP8X4), scales=wsc[a][:, lo:hi], in_=w_bf[a][:, PACK * lo : PACK * hi])

        xw = at(XG_AT, "xw", [P, S], U32)
        gather(xw[:], xw_win, offs_t[:])
        nc.scalar.activation(dst[0], src[0], COPY)
        quant_w(0, 0, H)
        nc.vector.tensor_scalar_mul(dst[1][:, :, :, 0:2], src[1][:, :, :, 0:2], -1.0)
        nc.vector.tensor_scalar_mul(dst[1][:, CUT:P, :, 2:4], src[1][:, CUT:P, :, 2:4], -1.0)
        nc.scalar.activation(dst[1][:, 0:CUT, :, 2:4], src[1][:, 0:CUT, :, 2:4], COPY, scale=-1.0)
        quant_w(1, 0, H // 2)
        quant_w(1, H // 2, H)
        hb = at(W2_AT, "hb", [P, V], F32)
        nc.scalar.copy(hb[:], spread[:].rearrange("p c n -> p (c n)"))
        ew = sb("ew", [P, S], U32)
        for lo, hi in ((0, P), (P, 2 * P), (2 * P, 3 * P), (3 * P, S)):
            gather(ew[:, lo:hi], ew_win, code_t[:, lo // 16 : hi // 16])

        rr_banks = [psum.tile([P, PACK, P], F32, name="rr_bank%d" % tt, tag="rr%d" % tt) for tt in range(4)]

        def passes(a, tt, first):
            cols = slice(tt * P, (tt + 1) * P)
            words = (xw, ew)[a][:, cols]
            for j in range(PACK):
                wc = slice(j * P, (j + 1) * P)
                nc.tensor.matmul_mx(out=rr_banks[tt][:, j, :], lhsT=wq[a][:, wc].bitcast(FP8X4), lhsT_scale=wsc[a][:, wc],
                                    rhs=words.bitcast(FP8X4), rhs_scale=planes[:, a, cols],
                                    start=(first and j == 0), stop=(not first and j == PACK - 1))

        AHEAD = 2
        for tt in range(AHEAD):
            passes(0, tt, True)
        rr_bf = []
        for tt in range(4):
            passes(1, tt, tt >= AHEAD)
            if tt >= AHEAD:
                passes(0, tt, False)
            rb = sb("rr_bf%d" % tt, [P, P, PACK], BF16)
            nc.scalar.copy(rb[:], rr_banks[tt][:].rearrange("p j n -> p n j"))
            rr_bf.append(rb)

        vw = [sb("vw0", [P, HV], U32), at(VW1_AT, "vw1", [P, HV], U32)]
        slots = at(RQ_AT, "slots", [P, 3 * P], U32)
        rq, rs = [], []
        res = [sb("res%d" % tt, [P, V], F32) for tt in range(4)]

        def gather_v(h):
            gather(vw[h][:], vw_win, cand_t[:, h * HV // 16 : (h + 1) * HV // 16])

        def quant_rr(tt):
            rq.append(slots[:, (tt % 3) * P : (tt % 3 + 1) * P])
            rs.append(sb("rs%d" % tt, [P, P], U8))
            nc.vector.quantize_mx(out=rq[tt].bitcast(FP8X4), scales=rs[tt][:], in_=rr_bf[tt][:].rearrange("p n j -> p (n j)"))

        def product(tt, cols, tag):
            ob = psum.tile([P, HV], F32, name="o_bank%d_%d" % (tt, cols.start), tag=tag)
            nc.tensor.matmul_mx(out=ob[:], lhsT=rq[tt].bitcast(FP8X4), lhsT_scale=rs[tt][:],
                                rhs=vw[cols.start // HV][:].bitcast(FP8X4), rhs_scale=plane_v[:, cols], start=True, stop=True)
            return ob

        def finish(tt, cols, ob):
            nc.vector.tensor_tensor(res[tt][:, cols], ob[:], hb[:, cols], SUB)
            nc.sync.dma_start(out[tt * P : (tt + 1) * P, cols], res[tt][:, cols])

        lo, hi = slice(0, HV), slice(HV, V)
        def finish_aside(tt, cols, ob):
            nc.scalar.copy(plain[:, cols], ob[:])
            nc.gpsimd.tensor_tensor(res[tt][:, cols], plain[:, cols], hb[:, cols], SUB)
            nc.scalar.dma_start(out[tt * P : (tt + 1) * P, cols], res[tt][:, cols])

        plain = sb("plain", [P, HV], F32)
        gather_v(0)
        quant_rr(0)
        gather_v(1)
        quant_rr(1)
        b0 = [product(0, lo, "o0"), product(0, hi, "o1")]
        b1 = [product(1, lo, "o2"), product(1, hi, "o3")]
        finish(0, lo, b0[0])
        quant_rr(2)
        b2 = [product(2, lo, "rr0"), product(2, hi, "rr1")]
        finish(0, hi, b0[1])
        quant_rr(3)
        b3 = [product(3, lo, "rr2"), product(3, hi, "rr3")]
        finish_aside(1, lo, b1[0])
        finish(1, hi, b1[1])
        for tt, b in ((2, b2), (3, b3)):
            finish(tt, lo, b[0])
            finish(tt, hi, b[1])
